import numpy as np
import ml_dtypes


def mxq(x, axis, fmt="e4m3"):
    dtype, down = {"e4m3": (ml_dtypes.float8_e4m3fn, 7), "e5m2": (ml_dtypes.float8_e5m2, 14)}[fmt]
    v = np.moveaxis(np.asarray(x, np.float32).astype(ml_dtypes.bfloat16).astype(np.float64), axis, -1)
    blocks = v.reshape(v.shape[:-1] + (-1, 32))
    amax = np.abs(blocks).max(-1, keepdims=True)
    byte = np.maximum(np.where(amax > 0, np.frexp(amax)[1] - 1 + 127, 0) - down, 1)
    scale = np.exp2(byte - 127.0)
    codes = (blocks / scale).astype(np.float32).astype(dtype).astype(np.float64)
    return np.moveaxis((codes * scale).reshape(v.shape), -1, axis)


WIDE = False


def mx_kscale(k):
    if not WIDE:
        return np.ones(k)
    levels = np.array([30, -30])
    if k % 512:
        return np.exp2(np.random.permutation(np.resize(levels, k // 32))).repeat(32)
    a = np.empty((k // 512, 16))
    for p in range(k // 512):
        a[p, :8] = np.random.permutation(np.resize(levels, 8))
        for g in range(8):
            far = levels[np.abs(levels - a[p, g]) >= 10]
            a[p, g + 8] = far[np.random.randint(len(far))]
    return np.exp2(a.ravel()).repeat(32)


BF16 = ml_dtypes.bfloat16


def bf(x):
    return np.asarray(x, np.float32).astype(BF16)


def f64(x):
    return np.asarray(x).astype(np.float64)


E2M1 = np.array([0.0, 0.5, 1.0, 1.5, 2.0, 3.0, 4.0, 6.0, -0.0, -0.5, -1.0, -1.5, -2.0, -3.0, -4.0, -6.0])


def pack_weight(w, fmt):
    k, n = w.shape
    w = f64(bf(w)).reshape(k // 32, 32, n)
    amax = np.abs(w).max(1)
    if fmt in ("e4m3", "e5m2"):
        byte = np.frexp(amax)[1] - 1 + 127 - (7 if fmt == "e4m3" else 14)
    else:
        mant, ex = np.frexp(amax / 6.0)
        byte = np.where(mant > 0.5, ex, ex - 1) + 127
    byte = np.clip(np.where(amax > 0, byte, 1), 1, 254)
    scaled = (w * np.exp2(127.0 - byte)[:, None, :]).reshape(k, n).astype(np.float32)
    by_word = np.ascontiguousarray(scaled.reshape(k // 512, 128, 4, n).transpose(0, 1, 3, 2))
    if fmt in ("e4m3", "e5m2"):
        words = by_word.astype(ml_dtypes.float8_e4m3fn if fmt == "e4m3" else ml_dtypes.float8_e5m2).view(np.uint8)
    else:
        c = by_word.astype(ml_dtypes.float4_e2m1fn).view(np.uint8) & 0xF
        words = c[..., 0::2] | (c[..., 1::2] << 4)
    return np.ascontiguousarray(words), np.ascontiguousarray(byte.astype(np.uint8).reshape(k // 512, 16, n))


def unpack_weight(words, scales, fmt):
    g, p, n, _ = words.shape
    if fmt in ("e4m3", "e5m2"):
        vals = np.ascontiguousarray(words).view(ml_dtypes.float8_e4m3fn if fmt == "e4m3" else ml_dtypes.float8_e5m2).astype(np.float64)
    else:
        nib = np.empty((g, p, n, 4), np.uint8)
        nib[..., 0::2] = words & 0xF
        nib[..., 1::2] = words >> 4
        vals = E2M1[nib]
    vals = vals * np.repeat(np.exp2(scales.astype(np.float64) - 127.0), 8, axis=1)[..., None]
    return vals.transpose(0, 1, 3, 2).reshape(g * 512, n)

def planes(Y):
    n, m = Y.shape
    b = f64(bf(Y)).reshape(n // 32, 32, m)
    amax = np.abs(b).max(1)
    byte = np.clip(np.where(amax > 0, np.frexp(amax)[1] - 1 + 127 - 7, 1), 1, 254)
    codes = (b * np.exp2(127.0 - byte)[:, None, :]).reshape(n, m).astype(np.float32).astype(ml_dtypes.float8_e4m3fn).view(np.uint8)
    words = codes.reshape(n // 512, 128, 4, m).transpose(0, 1, 3, 2)
    return np.ascontiguousarray(words), np.ascontiguousarray(byte.astype(np.uint8).reshape(n // 512, 16, m))


BINS, VOXELS, FRAMES = 3072, 2048, 512


def setup_inputs():
    t = mx_kscale(BINS)[:, None]
    system = np.exp(2.0 * np.random.randn(BINS, VOXELS) - 2.0 + 0.4 * np.random.randn(VOXELS)) / BINS
    sens = system.sum(axis=0)
    expected = 4.0 * np.exp(np.random.randn(BINS, FRAMES))
    counts = np.random.poisson(expected * np.exp(np.random.randn(BINS, FRAMES)))
    ratio_words, ratio_scales = pack_weight(counts / expected / t, "e5m2")
    image = 0.7 * np.exp(0.8 * np.random.randn(VOXELS) + 0.3 * np.random.randn(FRAMES, VOXELS))
    return {"ratio_words": ratio_words, "ratio_scales": ratio_scales,
            "system": bf(system * t), "sens": bf(sens), "image": bf(image)}


def reference(ratio_words, ratio_scales, system, sens, image):
    R = unpack_weight(ratio_words, ratio_scales, "e5m2")
    A = mxq(f64(system), 0, "e4m3")
    back = R.T @ A
    y = f64(image) * back / f64(sens)
    Y = y.T
    words, scales = planes(Y)
    return y, words, scales

@@ -1,0 +1,266 @@
+from contextlib import ExitStack
+
+import concourse.mybir as mybir
+from concourse.masks import make_identity
+
+BINS, VOXELS, FRAMES = 3072, 2048, 512
+FLOPS = 2 * BINS * VOXELS * FRAMES
+
+F32 = mybir.dt.float32
+BF16 = mybir.dt.bfloat16
+I32 = mybir.dt.int32
+U32 = mybir.dt.uint32
+U8 = mybir.dt.uint8
+E4M3X4 = mybir.dt.float8_e4m3fn_x4
+E5M2X4 = mybir.dt.float8_e5m2_x4
+MULT = mybir.AluOpType.mult
+
+P = 128
+PACK = 4
+SPAN = P * PACK
+PASSES = BINS // SPAN
+GROUPS = VOXELS // SPAN
+BLOCKS = FRAMES // P
+CHUNKS = GROUPS * PASSES
+
+VEC_M = [84] * 6 + [60] * 13 + [52] * 5
+AHEAD = 10
+RAW_BUFS = 12
+ACC_BANKS = 5
+TURN_BANKS = 3
+IMAGE_LOAD_AFTER = {4: 0, 8: 1, 10: 2, 16: 3}
+RATIO_LOAD_AFTER = {0: [0], 1: [1], 2: [2], 3: [3], 5: [4, 5]}
+IMAGE_TURN_BEFORE = {4: 0, 9: 1, 12: 2, 18: 3}
+HALF = FRAMES // 2
+
+
+def tile_mlem_ratio_update_k2_kernel(tc, ratio_words, ratio_scales, system, sens, image, out_0, out_1, out_2):
+    nc = tc.nc
+    with ExitStack() as ctx:
+        keep = ctx.enter_context(tc.tile_pool(name="keep", bufs=1))
+        raws = ctx.enter_context(tc.tile_pool(name="raws", bufs=RAW_BUFS))
+        work = ctx.enter_context(tc.tile_pool(name="work", bufs=4))
+        pair = ctx.enter_context(tc.tile_pool(name="pair", bufs=2))
+        psum = ctx.enter_context(tc.psum_pool(name="psum", bufs=1))
+        ctx.enter_context(tc.manual_schedule(engines={mybir.EngineType.SP}))
+
+        r_words = keep.tile([P, PASSES, FRAMES], U32, align_bytes=64)
+        r_scales = keep.tile([P, PASSES * FRAMES], U8, align_bytes=64)
+        sens_sb = keep.tile([P, GROUPS, PACK], BF16)
+        inv_sens = keep.tile([P, GROUPS * PACK], F32)
+        ident = keep.tile([P, P], F32)
+        y_words = keep.tile([P, GROUPS, FRAMES], U32, align_bytes=64)
+        y_scales = keep.tile([P, GROUPS, FRAMES], U8, align_bytes=64)
+
+        raw, grouped, codes, scales = {}, {}, {}, {}
+        image_sb, image_t, acc, y_t, y_rows, y_grouped = {}, {}, {}, {}, {}, {}
+        image_bank = {}
+        counts = {"acc": 0, "turn": 0}
+
+        def next_bank(kind, banks, shape):
+            tag = "%s%d" % (kind, counts[kind] % banks)
+            counts[kind] += 1
+            return psum.tile(shape, F32, name=tag, tag=tag)
+
+        def load_image(g):
+            image_sb[g] = pair.tile([P, BLOCKS, SPAN], BF16, name="image_sb")
+            nc.sync.dma_start(
+                out=image_sb[g][:],
+                in_=image[:, g * SPAN : (g + 1) * SPAN].rearrange("(i f) v -> f i v", f=P),
+            )
+
+        def load_chunk(n):
+            g, c = divmod(n, PASSES)
+            raw[n] = raws.tile([P, PACK, SPAN], BF16, name="raw")
+            nc.sync.dma_start(
+                out=raw[n][:],
+                in_=system[c * SPAN : (c + 1) * SPAN, g * SPAN : (g + 1) * SPAN].rearrange("(p j) w -> p j w", j=PACK),
+            )
+            if n == 0:
+                for q in range(4):
+                    nc.sync.dma_start(
+                        out=r_scales[32 * q : 32 * q + 4, :].bitcast(I32).rearrange("r (c n) -> r c n", c=PASSES),
+                        in_=ratio_scales[:, 4 * q : 4 * q + 4, :].bitcast(I32).rearrange("c r n -> r c n"),
+                    )
+            for k in RATIO_LOAD_AFTER.get(n, []):
+                nc.sync.dma_start(
+                    out=r_words[:, k, :].bitcast(I32),
+                    in_=ratio_words[k].rearrange("p n t -> p (n t)").bitcast(I32),
+                )
+            if n == 1:
+                nc.sync.dma_start(out=sens_sb[:], in_=sens.rearrange("(g p t) -> p g t", p=P, t=PACK))
+            if n in IMAGE_LOAD_AFTER:
+                load_image(IMAGE_LOAD_AFTER[n])
+
+        def interleave_views(n):
+            if n not in grouped:
+                grouped[n] = work.tile([P, PACK * SPAN], BF16, name="grouped", align_bytes=64)
+            dst = grouped[n][:].rearrange("p (t m j) -> p m j t", t=PACK, j=PACK)
+            src = raw[n][:].rearrange("p j (m t) -> p m j t", t=PACK)
+            return dst, src
+
+        def interleave_scalar(n):
+            dst, src = interleave_views(n)
+            nc.scalar.copy(out=dst[:, VEC_M[n] :], in_=src[:, VEC_M[n] :])
+
+        def interleave_vector(n):
+            dst, src = interleave_views(n)
+            nc.vector.tensor_copy(out=dst[:, : VEC_M[n]], in_=src[:, : VEC_M[n]])
+
+        def quantize(n):
+            codes[n] = work.tile([P, SPAN], U32, name="codes", align_bytes=64)
+            scales[n] = work.tile([P, SPAN], U8, name="scales", align_bytes=64)
+            nc.vector.quantize_mx(out=codes[n][:].bitcast(E4M3X4), scales=scales[n][:], in_=grouped[n][:])
+
+        def multiply(n):
+            g, c = divmod(n, PASSES)
+            for t in range(PACK):
+                if c == 0:
+                    acc[g, t] = next_bank("acc", ACC_BANKS, [P, FRAMES])
+                cols = slice(t * P, (t + 1) * P)
+                nc.tensor.matmul_mx(
+                    out=acc[g, t][:],
+                    lhsT=codes[n][:, cols].bitcast(E4M3X4),
+                    lhsT_scale=scales[n][:, cols],
+                    rhs=r_words[:, c, :].bitcast(E5M2X4),
+                    rhs_scale=r_scales[:, c * FRAMES : (c + 1) * FRAMES],
+                    start=(c == 0),
+                    stop=(c == PASSES - 1),
+                )
+
+        def turn_image(g):
+            pairs = image_sb[g][:].bitcast(F32)
+            for u in range(2):
+                image_bank[u] = next_bank("turn", TURN_BANKS, [P, FRAMES])
+                for i in range(BLOCKS):
+                    nc.tensor.transpose(image_bank[u][:, i * P : (i + 1) * P], pairs[:, i, u : SPAN // 2 : 2], ident[:])
+
+        def copy_image(g):
+            image_t[g] = pair.tile([P, 2, FRAMES], F32, name="image_t")
+            for u in range(2):
+                nc.scalar.copy(out=image_t[g][:, u, :], in_=image_bank[u][:])
+
+        def update(g, frames):
+            if g not in y_t:
+                y_t[g] = pair.tile([P, PACK, FRAMES], F32, name="y_t")
+            img = image_t[g][:].bitcast(BF16).rearrange("p u (f e) -> p u e f", e=2)
+            for t in range(PACK):
+                nc.vector.scalar_tensor_tensor(
+                    out=y_t[g][:, t, frames],
+                    in0=acc[g, t][:, frames],
+                    scalar=inv_sens[:, g * PACK + t : g * PACK + t + 1],
+                    in1=img[:, t // 2, t % 2, frames],
+                    op0=MULT,
+                    op1=MULT,
+                )
+
+        def turn_result(g, i):
+            if i == 0:
+                y_rows[g] = work.tile([P, BLOCKS, SPAN], F32, name="y_rows", bufs=3)
+            bank = next_bank("turn", TURN_BANKS, [P, PACK, P])
+            for t in range(PACK):
+                nc.tensor.transpose(bank[:, t, :], y_t[g][:, t, i * P : (i + 1) * P], ident[:])
+            nc.scalar.copy(
+                out=y_rows[g][:, i, :].rearrange("f (p t) -> f p t", t=PACK),
+                in_=bank[:].rearrange("f t p -> f p t"),
+            )
+
+        def store_rows(g, first, last):
+            nc.sync.dma_start(
+                out=out_0[first * P : last * P, g * SPAN : (g + 1) * SPAN].rearrange("(i f) v -> f i v", f=P),
+                in_=y_rows[g][:, first:last, :],
+            )
+
+        def round_result(g, frames):
+            if g not in y_grouped:
+                y_grouped[g] = pair.tile([P, FRAMES, PACK], BF16, name="y_grouped", align_bytes=64)
+            nc.vector.tensor_copy(
+                out=y_grouped[g][:, frames, :].rearrange("p (c i) t -> p c t i", i=4),
+                in_=y_t[g][:, :, frames].rearrange("p t (c i) -> p c t i", i=4),
+            )
+
+        def quantize_result(g, frames):
+            nc.vector.quantize_mx(
+                out=y_words[:, g, frames].bitcast(E4M3X4),
+                scales=y_scales[:, g, frames],
+                in_=y_grouped[g][:, frames, :].rearrange("p f t -> p (f t)"),
+            )
+
+        def store_words(g, frames):
+            nc.sync.dma_start(
+                out=out_1[g, :, frames, :].rearrange("p m t -> p (m t)").bitcast(I32),
+                in_=y_words[:, g, frames].bitcast(I32),
+            )
+
+        def store_scales(engine, first, last):
+            for q in range(4):
+                engine.dma_start(
+                    out=out_2[first:last, 4 * q : 4 * q + 4, :].bitcast(I32).rearrange("g r m -> r g m"),
+                    in_=y_scales[32 * q : 32 * q + 4, first:last, :].bitcast(I32),
+                )
+
+        everything = slice(0, FRAMES)
+        halves = [slice(0, HALF), slice(HALF, FRAMES)]
+
+        nc.vector.memset(r_scales[:].bitcast(U32), 0)
+        make_identity(nc, ident[:])
+        for n in range(AHEAD):
+            load_chunk(n)
+        for n in range(PASSES):
+            load_chunk(n + AHEAD)
+            interleave_scalar(n)
+            interleave_vector(n)
+            if n == 2:
+                nc.vector.reciprocal(out=inv_sens[:], in_=sens_sb[:].rearrange("p g t -> p (g t)"))
+            quantize(n)
+            if n in IMAGE_TURN_BEFORE:
+                turn_image(IMAGE_TURN_BEFORE[n])
+            multiply(n)
+            if n - 1 in IMAGE_TURN_BEFORE:
+                copy_image(IMAGE_TURN_BEFORE[n - 1])
+        update(0, everything)
+        interleave_scalar(PASSES)
+        interleave_vector(PASSES)
+        for n in range(PASSES, CHUNKS):
+            g, c = divmod(n, PASSES)
+            if n + AHEAD < CHUNKS:
+                load_chunk(n + AHEAD)
+            if n + 1 < CHUNKS:
+                if c != 1:
+                    interleave_scalar(n + 1)
+                if c == 0:
+                    interleave_scalar(n + 2)
+                interleave_vector(n + 1)
+            if n in IMAGE_TURN_BEFORE:
+                turn_image(IMAGE_TURN_BEFORE[n])
+                copy_image(IMAGE_TURN_BEFORE[n])
+            quantize(n)
+            if c == 0 and g > 1:
+                update(g - 1, everything)
+            if c == 1:
+                round_result(g - 1, everything)
+                turn_result(g - 1, 0)
+                turn_result(g - 1, 1)
+            if c == 2:
+                quantize_result(g - 1, everything)
+                turn_result(g - 1, 2)
+                turn_result(g - 1, 3)
+            multiply(n)
+            if c == 3:
+                store_rows(g - 1, 0, BLOCKS)
+                store_words(g - 1, everything)
+                if g == GROUPS - 1:
+                    store_scales(nc.sync, 0, g)
+        g = GROUPS - 1
+        for h in range(2):
+            update(g, halves[h])
+        for h in range(2):
+            round_result(g, halves[h])
+        for h in range(2):
+            quantize_result(g, halves[h])
+        for i in range(BLOCKS):
+            turn_result(g, i)
+            store_rows(g, i, i + 1)
+            if i >= 2:
+                store_words(g, halves[i - 2])
+        store_scales(nc.scalar, g, g + 1)

@@ -21,17 +21,37 @@ SPAN = P * PACK
 PASSES = BINS // SPAN
 GROUPS = VOXELS // SPAN
 BLOCKS = FRAMES // P
-CHUNKS = GROUPS * PASSES
+QUADS = 4
+SENS_COLS = VOXELS // P
+RUN = 4
+RUNS = SPAN // RUN
 
-VEC_M = [84] * 6 + [60] * 13 + [52] * 5
-AHEAD = 10
-RAW_BUFS = 12
-ACC_BANKS = 5
-TURN_BANKS = 3
-IMAGE_LOAD_AFTER = {4: 0, 8: 1, 10: 2, 16: 3}
-RATIO_LOAD_AFTER = {0: [0], 1: [1], 2: [2], 3: [3], 5: [4, 5]}
-IMAGE_TURN_BEFORE = {4: 0, 9: 1, 12: 2, 18: 3}
-HALF = FRAMES // 2
+WIDE = 2 * SPAN
+RAW_BUFS = 7
+GROUPED_BUFS = 6
+CODE_BUFS = 8
+
+BANK_NAMES = "abcdefgh"
+TURN_BANK = {(0, 0): 4, (0, 2): 5, (1, 0): 6, (1, 2): 7, (2, 0): 0, (2, 2): 1, (3, 0): 2, (3, 2): 3, (3, 3): 0}
+
+ORDER = (
+    [(g, c) for c in range(4) for g in (0, 1)]
+    + [(0, 4), (0, 5), (1, 4), (1, 5)]
+    + [(3, 0), (2, 0), (2, 1), (2, 2), (3, 1), (2, 3), (3, 2), (2, 4), (2, 5), (3, 3), (3, 4), (3, 5)]
+)
+FIRST_HALF = 2 * PASSES
+
+VECTOR_RUNS = {
+    **{(g, c): 24 for g in (0, 1) for c in range(1, 5)},
+    **{(g, 0): 100 for g in (0, 1)},
+    **{(g, 5): 56 for g in (0, 1)},
+    **{chunk: 58 for chunk in ((3, 0), (2, 0), (2, 1), (2, 2))},
+    **{chunk: 94 for chunk in ((3, 1), (2, 3), (3, 2), (2, 4))},
+    (2, 5): 100,
+    (3, 3): 0,
+    (3, 4): 0,
+    (3, 5): RUNS,
+}
 
 
 def tile_mlem_ratio_update_k2_kernel(tc, ratio_words, ratio_scales, system, sens, image, out_0, out_1, out_2):
@@ -39,228 +59,282 @@ def tile_mlem_ratio_update_k2_kernel(tc, ratio_words, ratio_scales, system, sens
     with ExitStack() as ctx:
         keep = ctx.enter_context(tc.tile_pool(name="keep", bufs=1))
         raws = ctx.enter_context(tc.tile_pool(name="raws", bufs=RAW_BUFS))
-        work = ctx.enter_context(tc.tile_pool(name="work", bufs=4))
+        work = ctx.enter_context(tc.tile_pool(name="work", bufs=GROUPED_BUFS))
         pair = ctx.enter_context(tc.tile_pool(name="pair", bufs=2))
         psum = ctx.enter_context(tc.psum_pool(name="psum", bufs=1))
-        ctx.enter_context(tc.manual_schedule(engines={mybir.EngineType.SP}))
+        ctx.enter_context(tc.manual_schedule())
 
         r_words = keep.tile([P, PASSES, FRAMES], U32, align_bytes=64)
         r_scales = keep.tile([P, PASSES * FRAMES], U8, align_bytes=64)
-        sens_sb = keep.tile([P, GROUPS, PACK], BF16)
-        inv_sens = keep.tile([P, GROUPS * PACK], F32)
+        sens_sb = keep.tile([P, SENS_COLS], BF16)
+        inv_sens = keep.tile([P, SENS_COLS], F32)
+        inv_rows = keep.tile([P, VOXELS], F32)
         ident = keep.tile([P, P], F32)
+        image_sb = keep.tile([P, BLOCKS, VOXELS], BF16)
+        y_rows = keep.tile([P, BLOCKS, VOXELS], F32)
         y_words = keep.tile([P, GROUPS, FRAMES], U32, align_bytes=64)
         y_scales = keep.tile([P, GROUPS, FRAMES], U8, align_bytes=64)
 
         raw, grouped, codes, scales = {}, {}, {}, {}
-        image_sb, image_t, acc, y_t, y_rows, y_grouped = {}, {}, {}, {}, {}, {}
-        image_bank = {}
-        counts = {"acc": 0, "turn": 0}
+        acc, sens_bank, y_bank, y_round, y_grouped = {}, {}, {}, {}, {}
 
-        def next_bank(kind, banks, shape):
-            tag = "%s%d" % (kind, counts[kind] % banks)
-            counts[kind] += 1
-            return psum.tile(shape, F32, name=tag, tag=tag)
+        def bank(k, shape):
+            return psum.tile(shape, F32, name="bank_" + BANK_NAMES[k], tag="bank_" + BANK_NAMES[k])
 
-        def load_image(g):
-            image_sb[g] = pair.tile([P, BLOCKS, SPAN], BF16, name="image_sb")
+        def voxels(g, g_end=None):
+            return slice(g * SPAN, (g + 1 if g_end is None else g_end) * SPAN)
+
+
+        def load_system(g, g_end, c):
+            if (g // 2, c) not in raw:
+                raw[g // 2, c] = raws.tile([P, PACK, WIDE], BF16, name="raw")
             nc.sync.dma_start(
-                out=image_sb[g][:],
-                in_=image[:, g * SPAN : (g + 1) * SPAN].rearrange("(i f) v -> f i v", f=P),
+                out=raw[g // 2, c][:, :, voxels(g % 2, g_end - g + g % 2)],
+                in_=system[c * SPAN : (c + 1) * SPAN, voxels(g, g_end)].rearrange("(p j) w -> p j w", j=PACK),
             )
 
-        def load_chunk(n):
-            g, c = divmod(n, PASSES)
-            raw[n] = raws.tile([P, PACK, SPAN], BF16, name="raw")
+        def load_image(i):
+            nc.sync.dma_start(out=image_sb[:, i, :], in_=image[i * P : (i + 1) * P, :])
+
+        def load_ratio(c):
             nc.sync.dma_start(
-                out=raw[n][:],
-                in_=system[c * SPAN : (c + 1) * SPAN, g * SPAN : (g + 1) * SPAN].rearrange("(p j) w -> p j w", j=PACK),
+                out=r_words[:, c, :].bitcast(I32),
+                in_=ratio_words[c].rearrange("p n t -> p (n t)").bitcast(I32),
             )
-            if n == 0:
-                for q in range(4):
-                    nc.sync.dma_start(
-                        out=r_scales[32 * q : 32 * q + 4, :].bitcast(I32).rearrange("r (c n) -> r c n", c=PASSES),
-                        in_=ratio_scales[:, 4 * q : 4 * q + 4, :].bitcast(I32).rearrange("c r n -> r c n"),
-                    )
-            for k in RATIO_LOAD_AFTER.get(n, []):
+
+        def load_ratio_scales():
+            for q in range(QUADS):
                 nc.sync.dma_start(
-                    out=r_words[:, k, :].bitcast(I32),
-                    in_=ratio_words[k].rearrange("p n t -> p (n t)").bitcast(I32),
+                    out=r_scales[32 * q : 32 * q + 4, :].bitcast(I32).rearrange("r (c n) -> r c n", c=PASSES),
+                    in_=ratio_scales[:, 4 * q : 4 * q + 4, :].bitcast(I32).rearrange("c r n -> r c n"),
                 )
-            if n == 1:
-                nc.sync.dma_start(out=sens_sb[:], in_=sens.rearrange("(g p t) -> p g t", p=P, t=PACK))
-            if n in IMAGE_LOAD_AFTER:
-                load_image(IMAGE_LOAD_AFTER[n])
 
-        def interleave_views(n):
-            if n not in grouped:
-                grouped[n] = work.tile([P, PACK * SPAN], BF16, name="grouped", align_bytes=64)
-            dst = grouped[n][:].rearrange("p (t m j) -> p m j t", t=PACK, j=PACK)
-            src = raw[n][:].rearrange("p j (m t) -> p m j t", t=PACK)
+
+        def spread_sens(k):
+            sens_bank[k] = bank(BLOCKS + k, [P, PACK, P])
+            for t in range(PACK):
+                col = PACK * k + t
+                nc.tensor.transpose(sens_bank[k][:, t, :], inv_sens[:, col : col + 1].to_broadcast([P, P]), ident[:])
+
+        def copy_sens(k):
+            nc.scalar.copy(
+                out=inv_rows[:].rearrange("f (p c) -> f p c", p=P)[:, :, PACK * k : PACK * (k + 1)],
+                in_=sens_bank[k][:].rearrange("f t p -> f p t"),
+            )
+
+        def weigh(g, i):
+            nc.vector.tensor_tensor(
+                out=y_rows[:, i, voxels(g)], in0=image_sb[:, i, voxels(g)], in1=inv_rows[:, voxels(g)], op=MULT
+            )
+
+
+        def interleave_views(g, c):
+            if (g, c) not in grouped:
+                grouped[g, c] = work.tile([P, SPAN, PACK], BF16, name="grouped", align_bytes=64)
+            dst = grouped[g, c][:].rearrange("p (c i) j -> p c j i", i=RUN)
+            src = raw[g // 2, c][:, :, voxels(g % 2)].rearrange("p j (c i) -> p c j i", i=RUN)
             return dst, src
 
-        def interleave_scalar(n):
-            dst, src = interleave_views(n)
-            nc.scalar.copy(out=dst[:, VEC_M[n] :], in_=src[:, VEC_M[n] :])
+        def interleave_scalar(g, c):
+            split = VECTOR_RUNS[g, c]
+            if split < RUNS:
+                dst, src = interleave_views(g, c)
+                nc.scalar.copy(out=dst[:, split:], in_=src[:, split:])
 
-        def interleave_vector(n):
-            dst, src = interleave_views(n)
-            nc.vector.tensor_copy(out=dst[:, : VEC_M[n]], in_=src[:, : VEC_M[n]])
+        def interleave_vector(g, c):
+            split = VECTOR_RUNS[g, c]
+            if split > 0:
+                dst, src = interleave_views(g, c)
+                nc.vector.tensor_copy(out=dst[:, :split], in_=src[:, :split])
 
-        def quantize(n):
-            codes[n] = work.tile([P, SPAN], U32, name="codes", align_bytes=64)
-            scales[n] = work.tile([P, SPAN], U8, name="scales", align_bytes=64)
-            nc.vector.quantize_mx(out=codes[n][:].bitcast(E4M3X4), scales=scales[n][:], in_=grouped[n][:])
+        def quantize(g, c):
+            codes[g, c] = work.tile([P, SPAN], U32, name="codes", bufs=CODE_BUFS, align_bytes=64)
+            scales[g, c] = work.tile([P, SPAN], U8, name="scales", bufs=CODE_BUFS, align_bytes=64)
+            nc.vector.quantize_mx(
+                out=codes[g, c][:].bitcast(E4M3X4),
+                scales=scales[g, c][:],
+                in_=grouped[g, c][:].rearrange("p w j -> p (w j)"),
+            )
 
-        def multiply(n):
-            g, c = divmod(n, PASSES)
-            for t in range(PACK):
+        def multiply(g, c):
+            for i in range(BLOCKS):
                 if c == 0:
-                    acc[g, t] = next_bank("acc", ACC_BANKS, [P, FRAMES])
-                cols = slice(t * P, (t + 1) * P)
+                    acc[g, i] = bank(BLOCKS * (g % 2) + i, [P, SPAN])
                 nc.tensor.matmul_mx(
-                    out=acc[g, t][:],
-                    lhsT=codes[n][:, cols].bitcast(E4M3X4),
-                    lhsT_scale=scales[n][:, cols],
-                    rhs=r_words[:, c, :].bitcast(E5M2X4),
-                    rhs_scale=r_scales[:, c * FRAMES : (c + 1) * FRAMES],
+                    out=acc[g, i][:],
+                    lhsT=r_words[:, c, i * P : (i + 1) * P].bitcast(E5M2X4),
+                    lhsT_scale=r_scales[:, c * FRAMES + i * P : c * FRAMES + (i + 1) * P],
+                    rhs=codes[g, c][:].bitcast(E4M3X4),
+                    rhs_scale=scales[g, c][:],
                     start=(c == 0),
                     stop=(c == PASSES - 1),
                 )
 
-        def turn_image(g):
-            pairs = image_sb[g][:].bitcast(F32)
-            for u in range(2):
-                image_bank[u] = next_bank("turn", TURN_BANKS, [P, FRAMES])
-                for i in range(BLOCKS):
-                    nc.tensor.transpose(image_bank[u][:, i * P : (i + 1) * P], pairs[:, i, u : SPAN // 2 : 2], ident[:])
 
-        def copy_image(g):
-            image_t[g] = pair.tile([P, 2, FRAMES], F32, name="image_t")
-            for u in range(2):
-                nc.scalar.copy(out=image_t[g][:, u, :], in_=image_bank[u][:])
+        def update(g, i):
+            rows = y_rows[:, i, voxels(g)]
+            nc.vector.tensor_tensor(out=rows, in0=acc[g, i][:], in1=rows, op=MULT)
 
-        def update(g, frames):
-            if g not in y_t:
-                y_t[g] = pair.tile([P, PACK, FRAMES], F32, name="y_t")
-            img = image_t[g][:].bitcast(BF16).rearrange("p u (f e) -> p u e f", e=2)
-            for t in range(PACK):
-                nc.vector.scalar_tensor_tensor(
-                    out=y_t[g][:, t, frames],
-                    in0=acc[g, t][:, frames],
-                    scalar=inv_sens[:, g * PACK + t : g * PACK + t + 1],
-                    in1=img[:, t // 2, t % 2, frames],
-                    op0=MULT,
-                    op1=MULT,
-                )
+        def round_rows(g, i):
+            if g not in y_round:
+                y_round[g] = pair.tile([P, BLOCKS, SPAN], BF16, name="y_round")
+            nc.scalar.copy(out=y_round[g][:, i, :], in_=y_rows[:, i, voxels(g)])
 
-        def turn_result(g, i):
-            if i == 0:
-                y_rows[g] = work.tile([P, BLOCKS, SPAN], F32, name="y_rows", bufs=3)
-            bank = next_bank("turn", TURN_BANKS, [P, PACK, P])
-            for t in range(PACK):
-                nc.tensor.transpose(bank[:, t, :], y_t[g][:, t, i * P : (i + 1) * P], ident[:])
-            nc.scalar.copy(
-                out=y_rows[g][:, i, :].rearrange("f (p t) -> f p t", t=PACK),
-                in_=bank[:].rearrange("f t p -> f p t"),
-            )
+        def update_rounded(g, i):
+            nc.vector.tensor_tensor(out=y_round[g][:, i, :], in0=acc[g, i][:], in1=y_rows[:, i, voxels(g)], op=MULT)
 
-        def store_rows(g, first, last):
-            nc.sync.dma_start(
-                out=out_0[first * P : last * P, g * SPAN : (g + 1) * SPAN].rearrange("(i f) v -> f i v", f=P),
-                in_=y_rows[g][:, first:last, :],
-            )
+        def turn(g, first, end):
+            y_bank[g, first] = bank(TURN_BANK[g, first], [P, 2, (end - first) * P])
+            pairs = y_round[g][:].bitcast(F32)
+            for i in range(first, end):
+                for u in range(2):
+                    nc.tensor.transpose(
+                        y_bank[g, first][:, u, (i - first) * P : (i - first + 1) * P],
+                        pairs[:, i, u : SPAN // 2 : 2],
+                        ident[:],
+                    )
 
-        def round_result(g, frames):
+        def join(g, first, end):
             if g not in y_grouped:
                 y_grouped[g] = pair.tile([P, FRAMES, PACK], BF16, name="y_grouped", align_bytes=64)
-            nc.vector.tensor_copy(
-                out=y_grouped[g][:, frames, :].rearrange("p (c i) t -> p c t i", i=4),
-                in_=y_t[g][:, :, frames].rearrange("p t (c i) -> p c t i", i=4),
+            nc.scalar.copy(
+                out=y_grouped[g][:, first * P : end * P, :].bitcast(F32),
+                in_=y_bank[g, first][:].rearrange("p u f -> p f u"),
             )
 
-        def quantize_result(g, frames):
+        def quantize_result(g, first, end):
+            frames = slice(first * P, end * P)
             nc.vector.quantize_mx(
                 out=y_words[:, g, frames].bitcast(E4M3X4),
                 scales=y_scales[:, g, frames],
                 in_=y_grouped[g][:, frames, :].rearrange("p f t -> p (f t)"),
             )
 
-        def store_words(g, frames):
+
+        def store_rows(g, g_end, first, end):
+            nc.sync.dma_start(
+                out=out_0[first * P : end * P, voxels(g, g_end)].rearrange("(i f) v -> f i v", f=P),
+                in_=y_rows[:, first:end, voxels(g, g_end)],
+            )
+
+        def store_words(g, first, end):
+            frames = slice(first * P, end * P)
             nc.sync.dma_start(
                 out=out_1[g, :, frames, :].rearrange("p m t -> p (m t)").bitcast(I32),
                 in_=y_words[:, g, frames].bitcast(I32),
             )
 
-        def store_scales(engine, first, last):
-            for q in range(4):
+        def store_scales(engine, g, g_end):
+            for q in range(QUADS):
                 engine.dma_start(
-                    out=out_2[first:last, 4 * q : 4 * q + 4, :].bitcast(I32).rearrange("g r m -> r g m"),
-                    in_=y_scales[32 * q : 32 * q + 4, first:last, :].bitcast(I32),
+                    out=out_2[g:g_end, 4 * q : 4 * q + 4, :].bitcast(I32).rearrange("g r m -> r g m"),
+                    in_=y_scales[32 * q : 32 * q + 4, g:g_end, :].bitcast(I32),
                 )
 
-        everything = slice(0, FRAMES)
-        halves = [slice(0, HALF), slice(HALF, FRAMES)]
+
+        def run(calls):
+            for call in calls:
+                call[0](*call[1:])
+
+        def step(s, before=(), between=(), after=()):
+            run(before)
+            if 0 < s < FIRST_HALF - 1:
+                interleave_scalar(*ORDER[s + 1])
+            if s >= FIRST_HALF:
+                interleave_scalar(*ORDER[s])
+            if s + 1 < len(ORDER):
+                interleave_vector(*ORDER[s + 1])
+            run(between)
+            quantize(*ORDER[s])
+            run(after)
 
         nc.vector.memset(r_scales[:].bitcast(U32), 0)
         make_identity(nc, ident[:])
-        for n in range(AHEAD):
-            load_chunk(n)
-        for n in range(PASSES):
-            load_chunk(n + AHEAD)
-            interleave_scalar(n)
-            interleave_vector(n)
-            if n == 2:
-                nc.vector.reciprocal(out=inv_sens[:], in_=sens_sb[:].rearrange("p g t -> p (g t)"))
-            quantize(n)
-            if n in IMAGE_TURN_BEFORE:
-                turn_image(IMAGE_TURN_BEFORE[n])
-            multiply(n)
-            if n - 1 in IMAGE_TURN_BEFORE:
-                copy_image(IMAGE_TURN_BEFORE[n - 1])
-        update(0, everything)
-        interleave_scalar(PASSES)
-        interleave_vector(PASSES)
-        for n in range(PASSES, CHUNKS):
-            g, c = divmod(n, PASSES)
-            if n + AHEAD < CHUNKS:
-                load_chunk(n + AHEAD)
-            if n + 1 < CHUNKS:
-                if c != 1:
-                    interleave_scalar(n + 1)
-                if c == 0:
-                    interleave_scalar(n + 2)
-                interleave_vector(n + 1)
-            if n in IMAGE_TURN_BEFORE:
-                turn_image(IMAGE_TURN_BEFORE[n])
-                copy_image(IMAGE_TURN_BEFORE[n])
-            quantize(n)
-            if c == 0 and g > 1:
-                update(g - 1, everything)
-            if c == 1:
-                round_result(g - 1, everything)
-                turn_result(g - 1, 0)
-                turn_result(g - 1, 1)
-            if c == 2:
-                quantize_result(g - 1, everything)
-                turn_result(g - 1, 2)
-                turn_result(g - 1, 3)
-            multiply(n)
-            if c == 3:
-                store_rows(g - 1, 0, BLOCKS)
-                store_words(g - 1, everything)
-                if g == GROUPS - 1:
-                    store_scales(nc.sync, 0, g)
-        g = GROUPS - 1
-        for h in range(2):
-            update(g, halves[h])
-        for h in range(2):
-            round_result(g, halves[h])
-        for h in range(2):
-            quantize_result(g, halves[h])
-        for i in range(BLOCKS):
-            turn_result(g, i)
-            store_rows(g, i, i + 1)
-            if i >= 2:
-                store_words(g, halves[i - 2])
-        store_scales(nc.scalar, g, g + 1)
+
+        nc.sync.dma_start(out=sens_sb[:], in_=sens.rearrange("(p c) -> p c", p=P))
+        load_system(0, 1, 0)
+        load_system(1, 2, 0)
+        for c in (1, 2):
+            load_image(c - 1)
+            load_system(0, 2, c)
+        load_image(2)
+        load_ratio_scales()
+        load_ratio(0)
+        load_system(0, 2, 3)
+        load_image(3)
+        load_ratio(1)
+        load_system(0, 2, 4)
+        load_ratio(2)
+        load_system(0, 1, 5)
+        load_ratio(3)
+        load_ratio(4)
+        load_system(1, 2, 5)
+        load_ratio(5)
+        for c in range(PASSES):
+            load_system(2, 4, c)
+
+        nc.vector.reciprocal(out=inv_sens[:], in_=sens_sb[:])
+        for k in range(SENS_COLS // PACK):
+            spread_sens(k)
+        copy_sens(0)
+        interleave_scalar(*ORDER[0])
+        interleave_vector(*ORDER[0])
+        copy_sens(1)
+        interleave_scalar(*ORDER[1])
+        copy_sens(2)
+        copy_sens(3)
+
+        weights = [(weigh, g, i) for i in range(BLOCKS) for g in range(GROUPS)]
+        for s in range(FIRST_HALF - 1):
+            mine = weights[2 * s - 2 : 2 * s] if s > 0 else []
+            matmuls = [] if ORDER[s] == (1, 3) else [(multiply, *ORDER[s])]
+            if ORDER[s] == (0, 5):
+                matmuls.append((multiply, 1, 3))
+            step(s, between=mine[:1], after=mine[1:] + matmuls)
+
+        step(
+            11,
+            before=[(update, 0, i) for i in range(BLOCKS)] + [(round_rows, 0, i) for i in range(3)],
+            after=[(multiply, 1, 5)],
+        )
+        step(12)
+        step(13, before=[(update, 1, 0), (round_rows, 0, 3)], between=[(update, 1, 1)])
+        step(14, before=[(update, 1, 2), (turn, 0, 0, 2)], between=[(update, 1, 3)], after=[(multiply, 2, 0)])
+        step(15, before=[(turn, 0, 2, 4), (join, 0, 0, 2)], after=[(multiply, 2, 1), (multiply, 2, 2)])
+        step(16)
+        step(17, before=[(round_rows, 1, i) for i in range(3)] + [(turn, 1, 0, 2)])
+        step(18, before=[(round_rows, 1, 3), (turn, 1, 2, 4), (join, 0, 2, 4)])
+        step(
+            19,
+            before=[(quantize_result, 0, 0, 4), (join, 1, 0, 2), (join, 1, 2, 4)],
+            after=[(multiply, 3, 0), (multiply, 2, 3), (multiply, 3, 1), (multiply, 2, 4)],
+        )
+        step(20, after=[(multiply, 2, 5), (multiply, 3, 2)])
+        step(21, before=[(quantize_result, 1, 0, 4)], after=[(multiply, 3, 3)])
+        store_rows(0, 2, 0, BLOCKS)
+        store_words(0, 0, BLOCKS)
+        store_words(1, 0, BLOCKS)
+        step(22, before=[(update, 2, i) for i in range(BLOCKS)])
+        store_rows(2, 3, 0, BLOCKS)
+        step(
+            23,
+            before=[(round_rows, 2, i) for i in range(BLOCKS)] + [(turn, 2, 0, 2), (turn, 2, 2, 4)],
+            after=[(multiply, 3, 4), (multiply, 3, 5), (join, 2, 0, 2), (join, 2, 2, 4), (quantize_result, 2, 0, 4)],
+        )
+        store_words(2, 0, BLOCKS)
+        store_scales(nc.sync, 0, 3)
+
+        last = GROUPS - 1
+        for i in range(BLOCKS - 1):
+            update(last, i)
+            round_rows(last, i)
+            store_rows(last, GROUPS, i, i + 1)
+        update_rounded(last, BLOCKS - 1)
+        update(last, BLOCKS - 1)
+        store_rows(last, GROUPS, BLOCKS - 1, BLOCKS)
+        for first, end in ((0, 2), (2, 3), (3, 4)):
+            turn(last, first, end)
+            join(last, first, end)
+            quantize_result(last, first, end)
+            store_words(last, first, end)
+        store_scales(nc.scalar, last, GROUPS)

from contextlib import ExitStack

import concourse.mybir as mybir
from concourse.masks import make_identity

BINS, VOXELS, FRAMES = 3072, 2048, 512
FLOPS = 2 * BINS * VOXELS * FRAMES

F32 = mybir.dt.float32
BF16 = mybir.dt.bfloat16
I32 = mybir.dt.int32
U32 = mybir.dt.uint32
U8 = mybir.dt.uint8
E4M3X4 = mybir.dt.float8_e4m3fn_x4
E5M2X4 = mybir.dt.float8_e5m2_x4
MULT = mybir.AluOpType.mult

P = 128
PACK = 4
SPAN = P * PACK
PASSES = BINS // SPAN
GROUPS = VOXELS // SPAN
BLOCKS = FRAMES // P
QUADS = 4
SENS_COLS = VOXELS // P
RUN = 4
RUNS = SPAN // RUN

WIDE = 2 * SPAN
RAW_BUFS = 7
GROUPED_BUFS = 6
CODE_BUFS = 8

BANK_NAMES = "abcdefgh"
TURN_BANK = {(0, 0): 4, (0, 2): 5, (1, 0): 6, (1, 2): 7, (2, 0): 0, (2, 2): 1, (3, 0): 2, (3, 2): 3, (3, 3): 0}

ORDER = (
    [(g, c) for c in range(4) for g in (0, 1)]
    + [(0, 4), (0, 5), (1, 4), (1, 5)]
    + [(3, 0), (2, 0), (2, 1), (2, 2), (3, 1), (2, 3), (3, 2), (2, 4), (2, 5), (3, 3), (3, 4), (3, 5)]
)
FIRST_HALF = 2 * PASSES

VECTOR_RUNS = {
    **{(g, c): 24 for g in (0, 1) for c in range(1, 5)},
    **{(g, 0): 100 for g in (0, 1)},
    **{(g, 5): 56 for g in (0, 1)},
    **{chunk: 58 for chunk in ((3, 0), (2, 0), (2, 1), (2, 2))},
    **{chunk: 94 for chunk in ((3, 1), (2, 3), (3, 2), (2, 4))},
    (2, 5): 100,
    (3, 3): 0,
    (3, 4): 0,
    (3, 5): RUNS,
}


def tile_mlem_ratio_update_k2_kernel(tc, ratio_words, ratio_scales, system, sens, image, out_0, out_1, out_2):
    nc = tc.nc
    with ExitStack() as ctx:
        keep = ctx.enter_context(tc.tile_pool(name="keep", bufs=1))
        raws = ctx.enter_context(tc.tile_pool(name="raws", bufs=RAW_BUFS))
        work = ctx.enter_context(tc.tile_pool(name="work", bufs=GROUPED_BUFS))
        pair = ctx.enter_context(tc.tile_pool(name="pair", bufs=2))
        psum = ctx.enter_context(tc.psum_pool(name="psum", bufs=1))
        ctx.enter_context(tc.manual_schedule())

        r_words = keep.tile([P, PASSES, FRAMES], U32, align_bytes=64)
        r_scales = keep.tile([P, PASSES * FRAMES], U8, align_bytes=64)
        sens_sb = keep.tile([P, SENS_COLS], BF16)
        inv_sens = keep.tile([P, SENS_COLS], F32)
        inv_rows = keep.tile([P, VOXELS], F32)
        ident = keep.tile([P, P], F32)
        image_sb = keep.tile([P, BLOCKS, VOXELS], BF16)
        y_rows = keep.tile([P, BLOCKS, VOXELS], F32)
        y_words = keep.tile([P, GROUPS, FRAMES], U32, align_bytes=64)
        y_scales = keep.tile([P, GROUPS, FRAMES], U8, align_bytes=64)

        raw, grouped, codes, scales = {}, {}, {}, {}
        acc, sens_bank, y_bank, y_round, y_grouped = {}, {}, {}, {}, {}

        def bank(k, shape):
            return psum.tile(shape, F32, name="bank_" + BANK_NAMES[k], tag="bank_" + BANK_NAMES[k])

        def voxels(g, g_end=None):
            return slice(g * SPAN, (g + 1 if g_end is None else g_end) * SPAN)


        def load_system(g, g_end, c):
            if (g // 2, c) not in raw:
                raw[g // 2, c] = raws.tile([P, PACK, WIDE], BF16, name="raw")
            nc.sync.dma_start(
                out=raw[g // 2, c][:, :, voxels(g % 2, g_end - g + g % 2)],
                in_=system[c * SPAN : (c + 1) * SPAN, voxels(g, g_end)].rearrange("(p j) w -> p j w", j=PACK),
            )

        def load_image(i):
            nc.sync.dma_start(out=image_sb[:, i, :], in_=image[i * P : (i + 1) * P, :])

        def load_ratio(c):
            nc.sync.dma_start(
                out=r_words[:, c, :].bitcast(I32),
                in_=ratio_words[c].rearrange("p n t -> p (n t)").bitcast(I32),
            )

        def load_ratio_scales():
            for q in range(QUADS):
                nc.sync.dma_start(
                    out=r_scales[32 * q : 32 * q + 4, :].bitcast(I32).rearrange("r (c n) -> r c n", c=PASSES),
                    in_=ratio_scales[:, 4 * q : 4 * q + 4, :].bitcast(I32).rearrange("c r n -> r c n"),
                )


        def spread_sens(k):
            sens_bank[k] = bank(BLOCKS + k, [P, PACK, P])
            for t in range(PACK):
                col = PACK * k + t
                nc.tensor.transpose(sens_bank[k][:, t, :], inv_sens[:, col : col + 1].to_broadcast([P, P]), ident[:])

        def copy_sens(k):
            nc.scalar.copy(
                out=inv_rows[:].rearrange("f (p c) -> f p c", p=P)[:, :, PACK * k : PACK * (k + 1)],
                in_=sens_bank[k][:].rearrange("f t p -> f p t"),
            )

        def weigh(g, i):
            nc.vector.tensor_tensor(
                out=y_rows[:, i, voxels(g)], in0=image_sb[:, i, voxels(g)], in1=inv_rows[:, voxels(g)], op=MULT
            )


        def interleave_views(g, c):
            if (g, c) not in grouped:
                grouped[g, c] = work.tile([P, SPAN, PACK], BF16, name="grouped", align_bytes=64)
            dst = grouped[g, c][:].rearrange("p (c i) j -> p c j i", i=RUN)
            src = raw[g // 2, c][:, :, voxels(g % 2)].rearrange("p j (c i) -> p c j i", i=RUN)
            return dst, src

        def interleave_scalar(g, c):
            split = VECTOR_RUNS[g, c]
            if split < RUNS:
                dst, src = interleave_views(g, c)
                nc.scalar.copy(out=dst[:, split:], in_=src[:, split:])

        def interleave_vector(g, c):
            split = VECTOR_RUNS[g, c]
            if split > 0:
                dst, src = interleave_views(g, c)
                nc.vector.tensor_copy(out=dst[:, :split], in_=src[:, :split])

        def quantize(g, c):
            codes[g, c] = work.tile([P, SPAN], U32, name="codes", bufs=CODE_BUFS, align_bytes=64)
            scales[g, c] = work.tile([P, SPAN], U8, name="scales", bufs=CODE_BUFS, align_bytes=64)
            nc.vector.quantize_mx(
                out=codes[g, c][:].bitcast(E4M3X4),
                scales=scales[g, c][:],
                in_=grouped[g, c][:].rearrange("p w j -> p (w j)"),
            )

        def multiply(g, c):
            for i in range(BLOCKS):
                if c == 0:
                    acc[g, i] = bank(BLOCKS * (g % 2) + i, [P, SPAN])
                nc.tensor.matmul_mx(
                    out=acc[g, i][:],
                    lhsT=r_words[:, c, i * P : (i + 1) * P].bitcast(E5M2X4),
                    lhsT_scale=r_scales[:, c * FRAMES + i * P : c * FRAMES + (i + 1) * P],
                    rhs=codes[g, c][:].bitcast(E4M3X4),
                    rhs_scale=scales[g, c][:],
                    start=(c == 0),
                    stop=(c == PASSES - 1),
                )


        def update(g, i):
            rows = y_rows[:, i, voxels(g)]
            nc.vector.tensor_tensor(out=rows, in0=acc[g, i][:], in1=rows, op=MULT)

        def round_rows(g, i):
            if g not in y_round:
                y_round[g] = pair.tile([P, BLOCKS, SPAN], BF16, name="y_round")
            nc.scalar.copy(out=y_round[g][:, i, :], in_=y_rows[:, i, voxels(g)])

        def update_rounded(g, i):
            nc.vector.tensor_tensor(out=y_round[g][:, i, :], in0=acc[g, i][:], in1=y_rows[:, i, voxels(g)], op=MULT)

        def turn(g, first, end):
            y_bank[g, first] = bank(TURN_BANK[g, first], [P, 2, (end - first) * P])
            pairs = y_round[g][:].bitcast(F32)
            for i in range(first, end):
                for u in range(2):
                    nc.tensor.transpose(
                        y_bank[g, first][:, u, (i - first) * P : (i - first + 1) * P],
                        pairs[:, i, u : SPAN // 2 : 2],
                        ident[:],
                    )

        def join(g, first, end):
            if g not in y_grouped:
                y_grouped[g] = pair.tile([P, FRAMES, PACK], BF16, name="y_grouped", align_bytes=64)
            nc.scalar.copy(
                out=y_grouped[g][:, first * P : end * P, :].bitcast(F32),
                in_=y_bank[g, first][:].rearrange("p u f -> p f u"),
            )

        def quantize_result(g, first, end):
            frames = slice(first * P, end * P)
            nc.vector.quantize_mx(
                out=y_words[:, g, frames].bitcast(E4M3X4),
                scales=y_scales[:, g, frames],
                in_=y_grouped[g][:, frames, :].rearrange("p f t -> p (f t)"),
            )


        def store_rows(g, g_end, first, end):
            nc.sync.dma_start(
                out=out_0[first * P : end * P, voxels(g, g_end)].rearrange("(i f) v -> f i v", f=P),
                in_=y_rows[:, first:end, voxels(g, g_end)],
            )

        def store_words(g, first, end):
            frames = slice(first * P, end * P)
            nc.sync.dma_start(
                out=out_1[g, :, frames, :].rearrange("p m t -> p (m t)").bitcast(I32),
                in_=y_words[:, g, frames].bitcast(I32),
            )

        def store_scales(engine, g, g_end):
            for q in range(QUADS):
                engine.dma_start(
                    out=out_2[g:g_end, 4 * q : 4 * q + 4, :].bitcast(I32).rearrange("g r m -> r g m"),
                    in_=y_scales[32 * q : 32 * q + 4, g:g_end, :].bitcast(I32),
                )


        def run(calls):
            for call in calls:
                call[0](*call[1:])

        def step(s, before=(), between=(), after=()):
            run(before)
            if 0 < s < FIRST_HALF - 1:
                interleave_scalar(*ORDER[s + 1])
            if s >= FIRST_HALF:
                interleave_scalar(*ORDER[s])
            if s + 1 < len(ORDER):
                interleave_vector(*ORDER[s + 1])
            run(between)
            quantize(*ORDER[s])
            run(after)

        nc.vector.memset(r_scales[:].bitcast(U32), 0)
        make_identity(nc, ident[:])

        nc.sync.dma_start(out=sens_sb[:], in_=sens.rearrange("(p c) -> p c", p=P))
        load_system(0, 1, 0)
        load_system(1, 2, 0)
        for c in (1, 2):
            load_image(c - 1)
            load_system(0, 2, c)
        load_image(2)
        load_ratio_scales()
        load_ratio(0)
        load_system(0, 2, 3)
        load_image(3)
        load_ratio(1)
        load_system(0, 2, 4)
        load_ratio(2)
        load_system(0, 1, 5)
        load_ratio(3)
        load_ratio(4)
        load_system(1, 2, 5)
        load_ratio(5)
        for c in range(PASSES):
            load_system(2, 4, c)

        nc.vector.reciprocal(out=inv_sens[:], in_=sens_sb[:])
        for k in range(SENS_COLS // PACK):
            spread_sens(k)
        copy_sens(0)
        interleave_scalar(*ORDER[0])
        interleave_vector(*ORDER[0])
        copy_sens(1)
        interleave_scalar(*ORDER[1])
        copy_sens(2)
        copy_sens(3)

        weights = [(weigh, g, i) for i in range(BLOCKS) for g in range(GROUPS)]
        for s in range(FIRST_HALF - 1):
            mine = weights[2 * s - 2 : 2 * s] if s > 0 else []
            matmuls = [] if ORDER[s] == (1, 3) else [(multiply, *ORDER[s])]
            if ORDER[s] == (0, 5):
                matmuls.append((multiply, 1, 3))
            step(s, between=mine[:1], after=mine[1:] + matmuls)

        step(
            11,
            before=[(update, 0, i) for i in range(BLOCKS)] + [(round_rows, 0, i) for i in range(3)],
            after=[(multiply, 1, 5)],
        )
        step(12)
        step(13, before=[(update, 1, 0), (round_rows, 0, 3)], between=[(update, 1, 1)])
        step(14, before=[(update, 1, 2), (turn, 0, 0, 2)], between=[(update, 1, 3)], after=[(multiply, 2, 0)])
        step(15, before=[(turn, 0, 2, 4), (join, 0, 0, 2)], after=[(multiply, 2, 1), (multiply, 2, 2)])
        step(16)
        step(17, before=[(round_rows, 1, i) for i in range(3)] + [(turn, 1, 0, 2)])
        step(18, before=[(round_rows, 1, 3), (turn, 1, 2, 4), (join, 0, 2, 4)])
        step(
            19,
            before=[(quantize_result, 0, 0, 4), (join, 1, 0, 2), (join, 1, 2, 4)],
            after=[(multiply, 3, 0), (multiply, 2, 3), (multiply, 3, 1), (multiply, 2, 4)],
        )
        step(20, after=[(multiply, 2, 5), (multiply, 3, 2)])
        step(21, before=[(quantize_result, 1, 0, 4)], after=[(multiply, 3, 3)])
        store_rows(0, 2, 0, BLOCKS)
        store_words(0, 0, BLOCKS)
        store_words(1, 0, BLOCKS)
        step(22, before=[(update, 2, i) for i in range(BLOCKS)])
        store_rows(2, 3, 0, BLOCKS)
        step(
            23,
            before=[(round_rows, 2, i) for i in range(BLOCKS)] + [(turn, 2, 0, 2), (turn, 2, 2, 4)],
            after=[(multiply, 3, 4), (multiply, 3, 5), (join, 2, 0, 2), (join, 2, 2, 4), (quantize_result, 2, 0, 4)],
        )
        store_words(2, 0, BLOCKS)
        store_scales(nc.sync, 0, 3)

        last = GROUPS - 1
        for i in range(BLOCKS - 1):
            update(last, i)
            round_rows(last, i)
            store_rows(last, GROUPS, i, i + 1)
        update_rounded(last, BLOCKS - 1)
        update(last, BLOCKS - 1)
        store_rows(last, GROUPS, BLOCKS - 1, BLOCKS)
        for first, end in ((0, 2), (2, 3), (3, 4)):
            turn(last, first, end)
            join(last, first, end)
            quantize_result(last, first, end)
            store_words(last, first, end)
        store_scales(nc.scalar, last, GROUPS)
